import numpy as np
import ml_dtypes


def mxq(x, axis, fmt="e4m3"):
    dtype, down = {"e4m3": (ml_dtypes.float8_e4m3fn, 7), "e5m2": (ml_dtypes.float8_e5m2, 14)}[fmt]
    v = np.moveaxis(np.asarray(x, np.float32).astype(ml_dtypes.bfloat16).astype(np.float64), axis, -1)
    blocks = v.reshape(v.shape[:-1] + (-1, 32))
    amax = np.abs(blocks).max(-1, keepdims=True)
    byte = np.maximum(np.where(amax > 0, np.frexp(amax)[1] - 1 + 127, 0) - down, 1)
    scale = np.exp2(byte - 127.0)
    codes = (blocks / scale).astype(np.float32).astype(dtype).astype(np.float64)
    return np.moveaxis((codes * scale).reshape(v.shape), -1, axis)


WIDE = False


def mx_kscale(k):
    if not WIDE:
        return np.ones(k)
    levels = np.array([10, -10, 5, -5, 0])
    if k % 512:
        return np.exp2(np.random.permutation(np.resize(levels, k // 32))).repeat(32)
    a = np.empty((k // 512, 16))
    for p in range(k // 512):
        a[p, :8] = np.random.permutation(np.resize(levels, 8))
        for g in range(8):
            far = levels[np.abs(levels - a[p, g]) >= 10]
            a[p, g + 8] = far[np.random.randint(len(far))]
    return np.exp2(a.ravel()).repeat(32)


def f64(x):
    return np.asarray(x).astype(np.float64)


def striped(idx):
    return np.tile(idx.reshape(-1, 16).T, (8, 1)).astype(np.uint16)


def unstriped(offs):
    return offs[:16].T.reshape(-1).astype(np.int64)


K, T, E, C, N = 1024, 1536, 24, 128, 128


def by_expert(wq, xq):
    return np.concatenate([wq[e].T @ xq[:, e * C:(e + 1) * C] for e in range(E)], axis=1)


def setup_inputs():
    n = np.random.standard_normal
    s = mx_kscale(K)[:, None]
    first = np.random.permutation(np.repeat(np.arange(E), T // E))
    second = (first + 1 + np.random.permutation(np.repeat(np.arange(E - 1), -(-T // (E - 1)))[:T])) % E
    while np.bincount(second, minlength=E).max() != T // E:
        load = np.bincount(second, minlength=E); hi, lo = int(load.argmax()), int(load.argmin())
        t = np.flatnonzero((second == hi) & (first != lo))[0]; second[t] = lo
    slot_token = np.empty(E * C, np.int64); pos = np.empty((2, T), np.int64); fill = np.zeros(E, np.int64)
    place = np.stack([np.random.permutation(C) for _ in range(E)])
    for r, deal in enumerate((first, second)):
        for t in np.random.permutation(T):
            e = deal[t]; j = e * C + place[e, fill[e]]; fill[e] += 1; slot_token[j] = t; pos[r, t] = j
    g = np.random.uniform(0.2, 0.8, T)
    return {
        "xT": (n((K, T)) * s).astype(np.float32),
        "w": (n((E + 1, K, N)) / np.sqrt(K) / s[None]).astype(np.float32),
        "b": (0.3 * n((N, E + 1))).astype(np.float32),
        "gate": np.stack([np.tile(g, (N, 1)), np.tile(1.0 - g, (N, 1))]).astype(np.float32),
        "offs": striped(slot_token),
        "pos1": striped(pos[0]),
        "pos2": striped(pos[1]),
    }


def reference(xT, w, b, gate, offs, pos1, pos2):
    idx = unstriped(offs)
    wq = mxq(f64(w), 1, "e4m3")
    xs = mxq(f64(xT), 0, "e4m3")
    ys = (wq[E].T @ xs) + f64(b)[:, E:]
    xq = mxq(f64(xT)[:, idx], 0, "e4m3")
    y = by_expert(wq, xq)
    y = y + np.repeat(f64(b)[:, :E], C, axis=1)
    return ys + f64(gate[0]) * y[:, unstriped(pos1)] + f64(gate[1]) * y[:, unstriped(pos2)]

@@ -1,0 +1,238 @@
+from contextlib import ExitStack
+
+import concourse.mybir as mybir
+
+P = 128
+K, T, E, C, N = 1024, 1536, 24, 128, 128
+S = E * C
+G = 2
+Q = 3
+SQ = S // Q
+
+F32 = mybir.dt.float32
+BF16 = mybir.dt.bfloat16
+U32 = mybir.dt.uint32
+U16 = mybir.dt.uint16
+U8 = mybir.dt.uint8
+FP8X4 = mybir.dt.float8_e4m3fn_x4
+ADD = mybir.AluOpType.add
+MULT = mybir.AluOpType.mult
+IDENTITY = mybir.ActivationFunctionType.Identity
+
+FLOPS = 2 * K * N * (S + T)
+
+W_VECTOR = (5,)
+XCUT = 768
+
+
+def tile_moe_shr_lin_bias_kernel(tc, xT, w, b, gate, offs, pos1, pos2, out):
+    nc = tc.nc
+    with ExitStack() as ctx:
+        held = ctx.enter_context(tc.tile_pool(name="held", bufs=1))
+        ring = ctx.enter_context(tc.tile_pool(name="ring", bufs=1))
+        psum = ctx.enter_context(tc.psum_pool(name="psum", bufs=1))
+
+        offs_t = held.tile([P, S // 16], U16, name="offs_t")
+        pos1_t = held.tile([P, T // 16], U16, name="pos1_t")
+        pos2_t = held.tile([P, T // 16], U16, name="pos2_t")
+        b_t = held.tile([P, E + 1], F32, name="b_t")
+        sc = held.tile([P, G, S], U32, name="sc", align_bytes=64)
+        ss = held.tile([P, G, S], U8, name="ss", align_bytes=64)
+        xc = held.tile([P, G, T], U32, name="xc", align_bytes=64)
+        xs = held.tile([P, G, T], U8, name="xs", align_bytes=64)
+        wc = held.tile([P, E + 1, G, N], U32, name="wc", align_bytes=64)
+        ws = held.tile([P, E + 1, G, N], U8, name="ws", align_bytes=64)
+
+        x_view = xT.rearrange("(g p j) t -> g p j t", g=G, j=4)
+        w_view = w.rearrange("e (g p j) n -> p e g j n", g=G, j=4)
+
+        nc.sync.dma_start(offs_t[:], offs)
+
+        tables = []
+        for g in range(G):
+            table = ring.tile([P, 2, 2 * T], BF16, name="table%d" % g, tag="t12", bufs=2, align_bytes=64)
+            tables.append(table)
+
+        def load_x(g, u, h):
+            raw = ring.tile([P, 2, XCUT], F32, name="xraw", tag="xraw", bufs=4, align_bytes=64)
+            nc.sync.dma_start(raw[:], x_view[g, :, 2 * u : 2 * u + 2, h * XCUT : (h + 1) * XCUT])
+            return raw
+
+        def cast_x(raw, g, u, h, on_vector):
+            dst = tables[g][:, u, 2 * h * XCUT : 2 * (h + 1) * XCUT].rearrange("p (n e) -> p n e", e=2)
+            src = raw[:].rearrange("p e n -> p n e")
+            if on_vector:
+                nc.vector.tensor_copy(dst, src)
+            else:
+                nc.scalar.copy(dst, src)
+
+        planes = {}
+
+        def gather(g, u, q):
+            if u == 0:
+                planes[g, q] = ring.tile([P, 2, 2 * SQ], BF16, name="planes", tag="planes", bufs=4, align_bytes=64)
+            nc.vector.tensor_copy(
+                planes[g, q][:, u, :].bitcast(U32),
+                tables[g][:, u, :].bitcast(U32).indirect(offs_t[:, q * SQ // 16 : (q + 1) * SQ // 16]),
+            )
+
+        grouped = {}
+
+        def interleave(g, q, on_vector):
+            t = ring.tile([P, 4 * SQ], BF16, name="grouped", tag="grouped", bufs=3, align_bytes=64)
+            dst = t[:].bitcast(F32).rearrange("p (n u) -> p n u", u=2)
+            src = planes[g, q][:].rearrange("p u m -> p (u m)").bitcast(F32).rearrange("p (u n) -> p n u", u=2)
+            if on_vector:
+                nc.vector.tensor_copy(dst, src)
+            else:
+                nc.scalar.copy(dst, src)
+            grouped[g, q] = t
+
+        def quantise_slots(g, q):
+            cols = slice(q * SQ, (q + 1) * SQ)
+            nc.vector.quantize_mx(out=sc[:, g, cols].bitcast(FP8X4), scales=ss[:, g, cols], in_=grouped[g, q][:])
+
+        def load_w(e0, n):
+            raw = ring.tile([P, n, G, 4 * N], F32, name="wraw", tag="wraw", bufs=3, align_bytes=64)
+            nc.sync.dma_start(
+                raw[:].rearrange("p e g (j n) -> p e g j n", j=4), w_view[:, e0 : e0 + n]
+            )
+            return raw
+
+        wgrouped = {}
+
+        def cast_w(raw, e0, n, on_vector):
+            t = ring.tile([P, n * G * 4 * N], BF16, name="wgrouped", tag="wgrouped", bufs=3, align_bytes=64)
+            dst = t[:].rearrange("p (a c i t) -> p a c t i", c=N // 4, i=4, t=4)
+            src = raw[:].rearrange("p e g (t c i) -> p (e g) c t i", t=4, i=4)
+            if on_vector:
+                nc.vector.tensor_copy(dst, src)
+            else:
+                nc.scalar.copy(dst, src)
+            wgrouped[e0] = t
+
+        def quantise_w(e0, n):
+            nc.vector.quantize_mx(
+                out=wc[:, e0 : e0 + n].rearrange("p e g n -> p (e g n)").bitcast(FP8X4),
+                scales=ws[:, e0 : e0 + n].rearrange("p e g n -> p (e g n)"),
+                in_=wgrouped[e0][:],
+            )
+
+        def multiply(bank, e, codes, scales, cols):
+            for g in range(G):
+                nc.tensor.matmul_mx(
+                    out=bank,
+                    lhsT=wc[:, e, g, :].bitcast(FP8X4),
+                    lhsT_scale=ws[:, e, g, :],
+                    rhs=codes[:, g, cols].bitcast(FP8X4),
+                    rhs_scale=scales[:, g, cols],
+                    start=(g == 0),
+                    stop=(g == G - 1),
+                )
+
+        order = [(g, u) for g in range(G) for u in range(2)]
+        for g, u in order:
+            for h in range(T // XCUT):
+                raw = load_x(g, u, h)
+                cast_x(raw, g, u, h, (g, u, h) == (0, 0, 0))
+        nc.sync.dma_start(b_t[:], b)
+        nc.sync.dma_start(pos1_t[:], pos1)
+        nc.sync.dma_start(pos2_t[:], pos2)
+
+        pairs = E // 2
+        wraw = {}
+
+        def w_steps(lo, hi):
+            for i in range(lo, hi):
+                raw = load_w(2 * i, 2)
+                cast_w(raw, 2 * i, 2, i in W_VECTOR)
+                if i > lo:
+                    quantise_w(2 * (i - 1), 2)
+            quantise_w(2 * (hi - 1), 2)
+
+        for u in range(2):
+            for q in range(Q):
+                gather(0, u, q)
+        for q in range(Q):
+            interleave(0, q, False)
+        w_steps(0, 2)
+        for q in range(Q):
+            gather(1, 0, q)
+            quantise_slots(0, q)
+        for q in range(Q):
+            gather(1, 1, q)
+            if q > 0:
+                interleave(1, q - 1, False)
+            if q > 1:
+                quantise_slots(1, q - 2)
+        interleave(1, Q - 1, False)
+        w_steps(2, 4)
+        for q in range(1, Q):
+            quantise_slots(1, q)
+
+        def group_tokens(g, t0, n):
+            t = ring.tile([P, 4 * n], BF16, name="xgrouped", tag="grouped", bufs=3, align_bytes=64)
+            nc.vector.tensor_copy(
+                t[:].bitcast(F32).rearrange("p (n u) -> p n u", u=2),
+                tables[g][:].rearrange("p u m -> p (u m)").bitcast(F32).rearrange("p (u n) -> p n u", u=2)[:, t0 : t0 + n, :],
+            )
+            return t
+
+        def quantise_tokens(t, g, t0, n):
+            cols = slice(t0, t0 + n)
+            nc.vector.quantize_mx(out=xc[:, g, cols].bitcast(FP8X4), scales=xs[:, g, cols], in_=t[:])
+
+        def token_steps(g):
+            a = group_tokens(g, 0, 1024)
+            c = group_tokens(g, 1024, 512)
+            quantise_tokens(a, g, 0, 1024)
+            quantise_tokens(c, g, 1024, 512)
+
+        token_steps(0)
+        y = ring.tile([P, S], F32, name="y", tag="t12", bufs=2, align_bytes=64)
+        gates = []
+
+        def expert_bank(i):
+            bank = psum.tile([P, 4 * C], F32, name="bank", tag="bank", bufs=4)
+            for k in range(4):
+                e = 4 * i + k
+                multiply(bank[:, k * C : (k + 1) * C], e, sc, ss, slice(e * C, (e + 1) * C))
+            for k in range(4):
+                e = 4 * i + k
+                nc.scalar.activation(
+                    y[:, e * C : (e + 1) * C], bank[:, k * C : (k + 1) * C], IDENTITY, bias=b_t[:, e : e + 1]
+                )
+
+        for i in range(4, pairs, 2):
+            w_steps(i, i + 2)
+            if i == 8:
+                for r in range(2):
+                    t = ring.tile([P, T], F32, name="gate%d" % r, tag="xraw", bufs=4, align_bytes=64)
+                    nc.sync.dma_start(t[:], gate[r])
+                    gates.append(t)
+                raw = load_w(E, 1)
+                cast_w(raw, E, 1, False)
+            expert_bank(i // 2 - 2)
+        expert_bank(4)
+        expert_bank(5)
+        token_steps(1)
+        quantise_w(E, 1)
+        shared = []
+        for c in range(3):
+            bank = psum.tile([P, 512], F32, name="shared%d" % c)
+            multiply(bank[:], E, xc, xs, slice(c * 512, (c + 1) * 512))
+            shared.append(bank)
+
+        for c in range(3):
+            cols = slice(c * 512, (c + 1) * 512)
+            lists = slice(c * 32, (c + 1) * 32)
+            t1 = ring.tile([P, 512], F32, name="t1", tag="t1", bufs=2)
+            t2 = ring.tile([P, 512], F32, name="t2", tag="t2", bufs=2)
+            o = ring.tile([P, 512], F32, name="o", tag="o", bufs=2)
+            nc.vector.tensor_tensor(t1[:], y[:].indirect(pos1_t[:, lists]), gates[0][:, cols], MULT)
+            nc.vector.tensor_tensor(t2[:], y[:].indirect(pos2_t[:, lists]), gates[1][:, cols], MULT)
+            nc.vector.scalar_tensor_tensor(
+                out=o[:], in0=shared[c][:], scalar=b_t[:, E : E + 1], in1=t1[:], op0=ADD, op1=ADD
+            )
+            nc.vector.tensor_tensor(o[:], o[:], t2[:], ADD)
+            nc.sync.dma_start(out[:, cols], o[:])

@@ -21,8 +21,8 @@ IDENTITY = mybir.ActivationFunctionType.Identity
 
 FLOPS = 2 * K * N * (S + T)
 
-W_VECTOR = (5,)
-XCUT = 768
+W_VECTOR = (10, 14, 18, 23)
+XCUT = 512
 
 
 def tile_moe_shr_lin_bias_kernel(tc, xT, w, b, gate, offs, pos1, pos2, out):
@@ -44,7 +44,8 @@ def tile_moe_shr_lin_bias_kernel(tc, xT, w, b, gate, offs, pos1, pos2, out):
         ws = held.tile([P, E + 1, G, N], U8, name="ws", align_bytes=64)
 
         x_view = xT.rearrange("(g p j) t -> g p j t", g=G, j=4)
-        w_view = w.rearrange("e (g p j) n -> p e g j n", g=G, j=4)
+        w_view = w.rearrange("e (g p j) n -> e p g j n", g=G, j=4)
+        gate_view = gate.rearrange("r p t -> p r t")
 
         nc.sync.dma_start(offs_t[:], offs)
 
@@ -53,15 +54,15 @@ def tile_moe_shr_lin_bias_kernel(tc, xT, w, b, gate, offs, pos1, pos2, out):
             table = ring.tile([P, 2, 2 * T], BF16, name="table%d" % g, tag="t12", bufs=2, align_bytes=64)
             tables.append(table)
 
-        def load_x(g, u, h):
-            raw = ring.tile([P, 2, XCUT], F32, name="xraw", tag="xraw", bufs=4, align_bytes=64)
-            nc.sync.dma_start(raw[:], x_view[g, :, 2 * u : 2 * u + 2, h * XCUT : (h + 1) * XCUT])
-            return raw
+        def raw_tile(name):
+            return ring.tile([P, 2, 512], F32, name=name, tag="raw", bufs=12, align_bytes=64)
 
-        def cast_x(raw, g, u, h, on_vector):
+        def load_and_cast_x(g, u, h, engine):
+            raw = raw_tile("xraw")
+            nc.sync.dma_start(raw[:], x_view[g, :, 2 * u : 2 * u + 2, h * XCUT : (h + 1) * XCUT])
             dst = tables[g][:, u, 2 * h * XCUT : 2 * (h + 1) * XCUT].rearrange("p (n e) -> p n e", e=2)
             src = raw[:].rearrange("p e n -> p n e")
-            if on_vector:
+            if engine == "V":
                 nc.vector.tensor_copy(dst, src)
             else:
                 nc.scalar.copy(dst, src)
@@ -78,44 +79,36 @@ def tile_moe_shr_lin_bias_kernel(tc, xT, w, b, gate, offs, pos1, pos2, out):
 
         grouped = {}
 
-        def interleave(g, q, on_vector):
+        def interleave(g, q):
             t = ring.tile([P, 4 * SQ], BF16, name="grouped", tag="grouped", bufs=3, align_bytes=64)
             dst = t[:].bitcast(F32).rearrange("p (n u) -> p n u", u=2)
             src = planes[g, q][:].rearrange("p u m -> p (u m)").bitcast(F32).rearrange("p (u n) -> p n u", u=2)
-            if on_vector:
-                nc.vector.tensor_copy(dst, src)
-            else:
-                nc.scalar.copy(dst, src)
+            nc.scalar.copy(dst, src)
             grouped[g, q] = t
 
         def quantise_slots(g, q):
             cols = slice(q * SQ, (q + 1) * SQ)
             nc.vector.quantize_mx(out=sc[:, g, cols].bitcast(FP8X4), scales=ss[:, g, cols], in_=grouped[g, q][:])
 
-        def load_w(e0, n):
-            raw = ring.tile([P, n, G, 4 * N], F32, name="wraw", tag="wraw", bufs=3, align_bytes=64)
-            nc.sync.dma_start(
-                raw[:].rearrange("p e g (j n) -> p e g j n", j=4), w_view[:, e0 : e0 + n]
-            )
-            return raw
-
         wgrouped = {}
 
-        def cast_w(raw, e0, n, on_vector):
-            t = ring.tile([P, n * G * 4 * N], BF16, name="wgrouped", tag="wgrouped", bufs=3, align_bytes=64)
-            dst = t[:].rearrange("p (a c i t) -> p a c t i", c=N // 4, i=4, t=4)
-            src = raw[:].rearrange("p e g (t c i) -> p (e g) c t i", t=4, i=4)
-            if on_vector:
+        def load_and_cast_w(e):
+            raw = raw_tile("wraw")
+            nc.sync.dma_start(raw[:].rearrange("p g (j n) -> p g j n", j=4), w_view[e])
+            if e % 2 == 0:
+                wgrouped[e // 2] = ring.tile([P, 2, G * 4 * N], BF16, name="wgrouped", tag="wgrouped", bufs=4, align_bytes=64)
+            dst = wgrouped[e // 2][:, e % 2, :].rearrange("p (a c i t) -> p a c t i", c=N // 4, i=4, t=4)
+            src = raw[:].rearrange("p g (t c i) -> p g c t i", t=4, i=4)
+            if e in W_VECTOR:
                 nc.vector.tensor_copy(dst, src)
             else:
                 nc.scalar.copy(dst, src)
-            wgrouped[e0] = t
 
-        def quantise_w(e0, n):
+        def quantise_w(e, n):
             nc.vector.quantize_mx(
-                out=wc[:, e0 : e0 + n].rearrange("p e g n -> p (e g n)").bitcast(FP8X4),
-                scales=ws[:, e0 : e0 + n].rearrange("p e g n -> p (e g n)"),
-                in_=wgrouped[e0][:],
+                out=wc[:, e : e + n].rearrange("p e g n -> p (e g n)").bitcast(FP8X4),
+                scales=ws[:, e : e + n].rearrange("p e g n -> p (e g n)"),
+                in_=wgrouped[e // 2][:, e % 2 : e % 2 + n, :].rearrange("p e m -> p (e m)"),
             )
 
         def multiply(bank, e, codes, scales, cols):
@@ -129,46 +122,6 @@ def tile_moe_shr_lin_bias_kernel(tc, xT, w, b, gate, offs, pos1, pos2, out):
                     start=(g == 0),
                     stop=(g == G - 1),
                 )
-
-        order = [(g, u) for g in range(G) for u in range(2)]
-        for g, u in order:
-            for h in range(T // XCUT):
-                raw = load_x(g, u, h)
-                cast_x(raw, g, u, h, (g, u, h) == (0, 0, 0))
-        nc.sync.dma_start(b_t[:], b)
-        nc.sync.dma_start(pos1_t[:], pos1)
-        nc.sync.dma_start(pos2_t[:], pos2)
-
-        pairs = E // 2
-        wraw = {}
-
-        def w_steps(lo, hi):
-            for i in range(lo, hi):
-                raw = load_w(2 * i, 2)
-                cast_w(raw, 2 * i, 2, i in W_VECTOR)
-                if i > lo:
-                    quantise_w(2 * (i - 1), 2)
-            quantise_w(2 * (hi - 1), 2)
-
-        for u in range(2):
-            for q in range(Q):
-                gather(0, u, q)
-        for q in range(Q):
-            interleave(0, q, False)
-        w_steps(0, 2)
-        for q in range(Q):
-            gather(1, 0, q)
-            quantise_slots(0, q)
-        for q in range(Q):
-            gather(1, 1, q)
-            if q > 0:
-                interleave(1, q - 1, False)
-            if q > 1:
-                quantise_slots(1, q - 2)
-        interleave(1, Q - 1, False)
-        w_steps(2, 4)
-        for q in range(1, Q):
-            quantise_slots(1, q)
 
         def group_tokens(g, t0, n):
             t = ring.tile([P, 4 * n], BF16, name="xgrouped", tag="grouped", bufs=3, align_bytes=64)
@@ -188,33 +141,68 @@ def tile_moe_shr_lin_bias_kernel(tc, xT, w, b, gate, offs, pos1, pos2, out):
             quantise_tokens(a, g, 0, 1024)
             quantise_tokens(c, g, 1024, 512)
 
-        token_steps(0)
-        y = ring.tile([P, S], F32, name="y", tag="t12", bufs=2, align_bytes=64)
-        gates = []
-
-        def expert_bank(i):
+        def expert_bank(e0, n):
             bank = psum.tile([P, 4 * C], F32, name="bank", tag="bank", bufs=4)
-            for k in range(4):
-                e = 4 * i + k
-                multiply(bank[:, k * C : (k + 1) * C], e, sc, ss, slice(e * C, (e + 1) * C))
-            for k in range(4):
-                e = 4 * i + k
+            for k in range(n):
+                cols = slice((e0 + k) * C, (e0 + k + 1) * C)
+                multiply(bank[:, k * C : (k + 1) * C], e0 + k, sc, ss, cols)
+            for k in range(n):
+                e = e0 + k
                 nc.scalar.activation(
                     y[:, e * C : (e + 1) * C], bank[:, k * C : (k + 1) * C], IDENTITY, bias=b_t[:, e : e + 1]
                 )
 
-        for i in range(4, pairs, 2):
-            w_steps(i, i + 2)
-            if i == 8:
-                for r in range(2):
-                    t = ring.tile([P, T], F32, name="gate%d" % r, tag="xraw", bufs=4, align_bytes=64)
-                    nc.sync.dma_start(t[:], gate[r])
+        for g in range(G):
+            for u in range(2):
+                for h in range(T // XCUT):
+                    load_and_cast_x(g, u, h, "V" if (g, u) == (0, 0) else "S")
+        nc.sync.dma_start(b_t[:], b)
+        nc.sync.dma_start(pos1_t[:], pos1)
+        nc.sync.dma_start(pos2_t[:], pos2)
+
+        for u in range(2):
+            for q in range(Q):
+                gather(0, u, q)
+        for q in range(Q):
+            interleave(0, q)
+        for e in range(4):
+            load_and_cast_w(e)
+        for q in range(Q):
+            gather(1, 0, q)
+            quantise_slots(0, q)
+        for q in range(Q):
+            gather(1, 1, q)
+            interleave(1, q)
+        quantise_w(0, 2)
+        quantise_w(2, 2)
+        for q in range(Q):
+            quantise_slots(1, q)
+        load_and_cast_w(4)
+        load_and_cast_w(5)
+        quantise_w(4, 2)
+        gates = []
+        y = None
+        for i in range(3, E // 2):
+            load_and_cast_w(2 * i)
+            load_and_cast_w(2 * i + 1)
+            if i == 9:
+                load_and_cast_w(E)
+                for c in range(3):
+                    t = raw_tile("gate")
+                    nc.sync.dma_start(t[:], gate_view[:, :, c * 512 : (c + 1) * 512])
                     gates.append(t)
-                raw = load_w(E, 1)
-                cast_w(raw, E, 1, False)
-            expert_bank(i // 2 - 2)
-        expert_bank(4)
-        expert_bank(5)
+            if i == E // 2 - 1:
+                quantise_w(2 * i, 1)
+                quantise_w(2 * i + 1, 1)
+            else:
+                quantise_w(2 * i, 2)
+            if i == 3:
+                token_steps(0)
+                y = ring.tile([P, S], F32, name="y", tag="t12", bufs=2, align_bytes=64)
+            if i % 2 == 1:
+                expert_bank(2 * (i - 3), 4)
+        expert_bank(20, 2)
+        expert_bank(22, 2)
         token_steps(1)
         quantise_w(E, 1)
         shared = []
@@ -229,8 +217,8 @@ def tile_moe_shr_lin_bias_kernel(tc, xT, w, b, gate, offs, pos1, pos2, out):
             t1 = ring.tile([P, 512], F32, name="t1", tag="t1", bufs=2)
             t2 = ring.tile([P, 512], F32, name="t2", tag="t2", bufs=2)
             o = ring.tile([P, 512], F32, name="o", tag="o", bufs=2)
-            nc.vector.tensor_tensor(t1[:], y[:].indirect(pos1_t[:, lists]), gates[0][:, cols], MULT)
-            nc.vector.tensor_tensor(t2[:], y[:].indirect(pos2_t[:, lists]), gates[1][:, cols], MULT)
+            nc.vector.tensor_tensor(t1[:], y[:].indirect(pos1_t[:, lists]), gates[c][:, 0, :], MULT)
+            nc.vector.tensor_tensor(t2[:], y[:].indirect(pos2_t[:, lists]), gates[c][:, 1, :], MULT)
             nc.vector.scalar_tensor_tensor(
                 out=o[:], in0=shared[c][:], scalar=b_t[:, E : E + 1], in1=t1[:], op0=ADD, op1=ADD
             )

@@ -21,8 +21,7 @@ IDENTITY = mybir.ActivationFunctionType.Identity
 
 FLOPS = 2 * K * N * (S + T)
 
-W_VECTOR = (10, 14, 18, 23)
-XCUT = 512
+W_VECTOR = (8, 16, 23)
 
 
 def tile_moe_shr_lin_bias_kernel(tc, xT, w, b, gate, offs, pos1, pos2, out):
@@ -44,7 +43,7 @@ def tile_moe_shr_lin_bias_kernel(tc, xT, w, b, gate, offs, pos1, pos2, out):
         ws = held.tile([P, E + 1, G, N], U8, name="ws", align_bytes=64)
 
         x_view = xT.rearrange("(g p j) t -> g p j t", g=G, j=4)
-        w_view = w.rearrange("e (g p j) n -> e p g j n", g=G, j=4)
+        w_view = w.rearrange("e (g p j) n -> p e g j n", g=G, j=4)
         gate_view = gate.rearrange("r p t -> p r t")
 
         nc.sync.dma_start(offs_t[:], offs)
@@ -54,18 +53,19 @@ def tile_moe_shr_lin_bias_kernel(tc, xT, w, b, gate, offs, pos1, pos2, out):
             table = ring.tile([P, 2, 2 * T], BF16, name="table%d" % g, tag="t12", bufs=2, align_bytes=64)
             tables.append(table)
 
-        def raw_tile(name):
-            return ring.tile([P, 2, 512], F32, name=name, tag="raw", bufs=12, align_bytes=64)
+        def raw_tile(name, width):
+            return ring.tile([P, 2, width], F32, name=name, tag="raw", bufs=7, align_bytes=64)
 
-        def load_and_cast_x(g, u, h, engine):
-            raw = raw_tile("xraw")
-            nc.sync.dma_start(raw[:], x_view[g, :, 2 * u : 2 * u + 2, h * XCUT : (h + 1) * XCUT])
-            dst = tables[g][:, u, 2 * h * XCUT : 2 * (h + 1) * XCUT].rearrange("p (n e) -> p n e", e=2)
-            src = raw[:].rearrange("p e n -> p n e")
-            if engine == "V":
-                nc.vector.tensor_copy(dst, src)
-            else:
-                nc.scalar.copy(dst, src)
+        def load_and_cast_x(g, u, t0, width, cut, engine):
+            raw = raw_tile("xraw", width)
+            for c in range(0, width, cut):
+                nc.sync.dma_start(raw[:, :, c : c + cut], x_view[g, :, 2 * u : 2 * u + 2, t0 + c : t0 + c + cut])
+                dst = tables[g][:, u, 2 * (t0 + c) : 2 * (t0 + c + cut)].rearrange("p (n e) -> p n e", e=2)
+                src = raw[:, :, c : c + cut].rearrange("p e n -> p n e")
+                if engine == "V":
+                    nc.vector.tensor_copy(dst, src)
+                else:
+                    nc.scalar.copy(dst, src)
 
         planes = {}
 
@@ -92,23 +92,25 @@ def tile_moe_shr_lin_bias_kernel(tc, xT, w, b, gate, offs, pos1, pos2, out):
 
         wgrouped = {}
 
-        def load_and_cast_w(e):
-            raw = raw_tile("wraw")
-            nc.sync.dma_start(raw[:].rearrange("p g (j n) -> p g j n", j=4), w_view[e])
-            if e % 2 == 0:
-                wgrouped[e // 2] = ring.tile([P, 2, G * 4 * N], BF16, name="wgrouped", tag="wgrouped", bufs=4, align_bytes=64)
-            dst = wgrouped[e // 2][:, e % 2, :].rearrange("p (a c i t) -> p a c t i", c=N // 4, i=4, t=4)
-            src = raw[:].rearrange("p g (t c i) -> p g c t i", t=4, i=4)
-            if e in W_VECTOR:
-                nc.vector.tensor_copy(dst, src)
-            else:
-                nc.scalar.copy(dst, src)
+        def load_and_cast_w(e0, n, split):
+            raw = raw_tile("wraw", n * 4 * N)
+            halves = raw[:].rearrange("p a b -> p (a b)").rearrange("p (e g m) -> p e g m", g=G, m=4 * N)
+            nc.sync.dma_start(halves.rearrange("p e g (j n) -> p e g j n", j=4), w_view[:, e0 : e0 + n])
+            t = ring.tile([P, n, G * 4 * N], BF16, name="wgrouped", tag="wgrouped", bufs=5, align_bytes=64)
+            for k in range(0, n, split):
+                dst = t[:, k : k + split, :].rearrange("p e (a c i t) -> p (e a) c t i", c=N // 4, i=4, t=4)
+                src = halves[:, k : k + split].rearrange("p e g (t c i) -> p (e g) c t i", t=4, i=4)
+                if e0 + k in W_VECTOR:
+                    nc.vector.tensor_copy(dst, src)
+                else:
+                    nc.scalar.copy(dst, src)
+            wgrouped[e0] = t
 
-        def quantise_w(e, n):
+        def quantise_w(e0, n, k=0):
             nc.vector.quantize_mx(
-                out=wc[:, e : e + n].rearrange("p e g n -> p (e g n)").bitcast(FP8X4),
-                scales=ws[:, e : e + n].rearrange("p e g n -> p (e g n)"),
-                in_=wgrouped[e // 2][:, e % 2 : e % 2 + n, :].rearrange("p e m -> p (e m)"),
+                out=wc[:, e0 + k : e0 + k + n].rearrange("p e g n -> p (e g n)").bitcast(FP8X4),
+                scales=ws[:, e0 + k : e0 + k + n].rearrange("p e g n -> p (e g n)"),
+                in_=wgrouped[e0][:, k : k + n, :].rearrange("p e m -> p (e m)"),
             )
 
         def multiply(bank, e, codes, scales, cols):
@@ -123,21 +125,23 @@ def tile_moe_shr_lin_bias_kernel(tc, xT, w, b, gate, offs, pos1, pos2, out):
                     stop=(g == G - 1),
                 )
 
-        def group_tokens(g, t0, n):
+        def group_tokens(g, t0, n, on_vector):
             t = ring.tile([P, 4 * n], BF16, name="xgrouped", tag="grouped", bufs=3, align_bytes=64)
-            nc.vector.tensor_copy(
-                t[:].bitcast(F32).rearrange("p (n u) -> p n u", u=2),
-                tables[g][:].rearrange("p u m -> p (u m)").bitcast(F32).rearrange("p (u n) -> p n u", u=2)[:, t0 : t0 + n, :],
-            )
+            dst = t[:].bitcast(F32).rearrange("p (n u) -> p n u", u=2)
+            words = tables[g][:].rearrange("p u m -> p (u m)").bitcast(F32).rearrange("p (u n) -> p n u", u=2)
+            if on_vector:
+                nc.vector.tensor_copy(dst, words[:, t0 : t0 + n, :])
+            else:
+                nc.scalar.copy(dst, words[:, t0 : t0 + n, :])
             return t
 
         def quantise_tokens(t, g, t0, n):
             cols = slice(t0, t0 + n)
             nc.vector.quantize_mx(out=xc[:, g, cols].bitcast(FP8X4), scales=xs[:, g, cols], in_=t[:])
 
-        def token_steps(g):
-            a = group_tokens(g, 0, 1024)
-            c = group_tokens(g, 1024, 512)
+        def token_steps(g, on_vector):
+            a = group_tokens(g, 0, 1024, on_vector)
+            c = group_tokens(g, 1024, 512, on_vector)
             quantise_tokens(a, g, 0, 1024)
             quantise_tokens(c, g, 1024, 512)
 
@@ -152,10 +156,14 @@ def tile_moe_shr_lin_bias_kernel(tc, xT, w, b, gate, offs, pos1, pos2, out):
                     y[:, e * C : (e + 1) * C], bank[:, k * C : (k + 1) * C], IDENTITY, bias=b_t[:, e : e + 1]
                 )
 
-        for g in range(G):
-            for u in range(2):
-                for h in range(T // XCUT):
-                    load_and_cast_x(g, u, h, "V" if (g, u) == (0, 0) else "S")
+        load_and_cast_x(0, 0, 0, 1024, 512, "V")
+        load_and_cast_x(0, 0, 1024, 512, 256, "V")
+        load_and_cast_x(0, 1, 0, 1024, 512, "S")
+        load_and_cast_x(0, 1, 1024, 512, 512, "S")
+        load_and_cast_x(1, 0, 0, 1024, 1024, "S")
+        load_and_cast_x(1, 0, 1024, 512, 512, "S")
+        load_and_cast_x(1, 1, 0, 1024, 1024, "S")
+        load_and_cast_x(1, 1, 1024, 512, 512, "S")
         nc.sync.dma_start(b_t[:], b)
         nc.sync.dma_start(pos1_t[:], pos1)
         nc.sync.dma_start(pos2_t[:], pos2)
@@ -165,45 +173,43 @@ def tile_moe_shr_lin_bias_kernel(tc, xT, w, b, gate, offs, pos1, pos2, out):
                 gather(0, u, q)
         for q in range(Q):
             interleave(0, q)
-        for e in range(4):
-            load_and_cast_w(e)
+        pairs = E // 2
+        gates = []
+        cuts = ((0, 1024), (1024, 1536))
+        for i in range(3):
+            load_and_cast_w(2 * i, 2, 2)
+        for i in range(2):
+            quantise_w(2 * i, 2)
         for q in range(Q):
             gather(1, 0, q)
-            quantise_slots(0, q)
-        for q in range(Q):
             gather(1, 1, q)
             interleave(1, q)
-        quantise_w(0, 2)
-        quantise_w(2, 2)
+            quantise_slots(0, q)
+            load_and_cast_w(2 * (3 + q), 2, 2)
+            quantise_w(2 * (2 + q), 2)
         for q in range(Q):
             quantise_slots(1, q)
-        load_and_cast_w(4)
-        load_and_cast_w(5)
-        quantise_w(4, 2)
-        gates = []
-        y = None
-        for i in range(3, E // 2):
-            load_and_cast_w(2 * i)
-            load_and_cast_w(2 * i + 1)
+        token_steps(0, True)
+        y = ring.tile([P, S], F32, name="y", tag="t12", bufs=2, align_bytes=64)
+        for i in range(6, pairs):
             if i == 9:
-                load_and_cast_w(E)
-                for c in range(3):
-                    t = raw_tile("gate")
-                    nc.sync.dma_start(t[:], gate_view[:, :, c * 512 : (c + 1) * 512])
+                load_and_cast_w(E, 1, 1)
+                for t0, t1 in cuts:
+                    t = raw_tile("gates", t1 - t0)
+                    nc.sync.dma_start(t[:], gate_view[:, :, t0:t1])
                     gates.append(t)
-            if i == E // 2 - 1:
-                quantise_w(2 * i, 1)
-                quantise_w(2 * i + 1, 1)
-            else:
-                quantise_w(2 * i, 2)
-            if i == 3:
-                token_steps(0)
-                y = ring.tile([P, S], F32, name="y", tag="t12", bufs=2, align_bytes=64)
-            if i % 2 == 1:
+            load_and_cast_w(2 * i, 2, 2 if i < pairs - 1 else 1)
+            quantise_w(2 * (i - 1), 2)
+            if i == 6:
+                expert_bank(0, 4)
+                expert_bank(4, 4)
+            elif i % 2 == 1:
                 expert_bank(2 * (i - 3), 4)
+        quantise_w(E - 2, 1)
+        quantise_w(E - 2, 1, 1)
         expert_bank(20, 2)
         expert_bank(22, 2)
-        token_steps(1)
+        token_steps(1, True)
         quantise_w(E, 1)
         shared = []
         for c in range(3):
@@ -211,16 +217,37 @@ def tile_moe_shr_lin_bias_kernel(tc, xT, w, b, gate, offs, pos1, pos2, out):
             multiply(bank[:], E, xc, xs, slice(c * 512, (c + 1) * 512))
             shared.append(bank)
 
-        for c in range(3):
-            cols = slice(c * 512, (c + 1) * 512)
-            lists = slice(c * 32, (c + 1) * 32)
-            t1 = ring.tile([P, 512], F32, name="t1", tag="t1", bufs=2)
-            t2 = ring.tile([P, 512], F32, name="t2", tag="t2", bufs=2)
-            o = ring.tile([P, 512], F32, name="o", tag="o", bufs=2)
-            nc.vector.tensor_tensor(t1[:], y[:].indirect(pos1_t[:, lists]), gates[c][:, 0, :], MULT)
-            nc.vector.tensor_tensor(t2[:], y[:].indirect(pos2_t[:, lists]), gates[c][:, 1, :], MULT)
+        first = ring.tile([P, T], F32, name="first", tag="planes", bufs=4, align_bytes=64)
+        second = ring.tile([P, T], F32, name="second", tag="planes", bufs=4, align_bytes=64)
+        total = ring.tile([P, T], F32, name="total", tag="planes", bufs=4, align_bytes=64)
+
+        def fetch(dst, pos, r, k):
+            t0, t1 = cuts[k]
+            nc.vector.tensor_tensor(dst[:, t0:t1], y[:].indirect(pos[:, t0 // 16 : t1 // 16]), gates[k][:, r, :], MULT)
+
+        def add_shared(t0, t1):
+            c = t0 // 512
             nc.vector.scalar_tensor_tensor(
-                out=o[:], in0=shared[c][:], scalar=b_t[:, E : E + 1], in1=t1[:], op0=ADD, op1=ADD
+                out=total[:, t0:t1],
+                in0=shared[c][:, t0 - 512 * c : t1 - 512 * c],
+                scalar=b_t[:, E : E + 1],
+                in1=first[:, t0:t1],
+                op0=ADD,
+                op1=ADD,
             )
-            nc.vector.tensor_tensor(o[:], o[:], t2[:], ADD)
-            nc.sync.dma_start(out[:, cols], o[:])
+
+        def add_second(t0, t1):
+            nc.vector.tensor_tensor(total[:, t0:t1], total[:, t0:t1], second[:, t0:t1], ADD)
+            nc.sync.dma_start(out[:, t0:t1], total[:, t0:t1])
+
+        fetch(first, pos1_t, 0, 0)
+        fetch(second, pos2_t, 1, 0)
+        add_shared(0, 512)
+        add_shared(512, 1024)
+        fetch(first, pos1_t, 0, 1)
+        add_second(0, 1024)
+        fetch(second, pos2_t, 1, 1)
+        add_shared(1024, 1280)
+        add_shared(1280, 1536)
+        add_second(1024, 1280)
+        add_second(1280, 1536)

from contextlib import ExitStack

import concourse.mybir as mybir

P = 128
K, T, E, C, N = 1024, 1536, 24, 128, 128
S = E * C
G = 2
Q = 3
SQ = S // Q

F32 = mybir.dt.float32
BF16 = mybir.dt.bfloat16
U32 = mybir.dt.uint32
U16 = mybir.dt.uint16
U8 = mybir.dt.uint8
FP8X4 = mybir.dt.float8_e4m3fn_x4
ADD = mybir.AluOpType.add
MULT = mybir.AluOpType.mult
IDENTITY = mybir.ActivationFunctionType.Identity

FLOPS = 2 * K * N * (S + T)

W_VECTOR = (8, 16, 23)


def tile_moe_shr_lin_bias_kernel(tc, xT, w, b, gate, offs, pos1, pos2, out):
    nc = tc.nc
    with ExitStack() as ctx:
        held = ctx.enter_context(tc.tile_pool(name="held", bufs=1))
        ring = ctx.enter_context(tc.tile_pool(name="ring", bufs=1))
        psum = ctx.enter_context(tc.psum_pool(name="psum", bufs=1))

        offs_t = held.tile([P, S // 16], U16, name="offs_t")
        pos1_t = held.tile([P, T // 16], U16, name="pos1_t")
        pos2_t = held.tile([P, T // 16], U16, name="pos2_t")
        b_t = held.tile([P, E + 1], F32, name="b_t")
        sc = held.tile([P, G, S], U32, name="sc", align_bytes=64)
        ss = held.tile([P, G, S], U8, name="ss", align_bytes=64)
        xc = held.tile([P, G, T], U32, name="xc", align_bytes=64)
        xs = held.tile([P, G, T], U8, name="xs", align_bytes=64)
        wc = held.tile([P, E + 1, G, N], U32, name="wc", align_bytes=64)
        ws = held.tile([P, E + 1, G, N], U8, name="ws", align_bytes=64)

        x_view = xT.rearrange("(g p j) t -> g p j t", g=G, j=4)
        w_view = w.rearrange("e (g p j) n -> p e g j n", g=G, j=4)
        gate_view = gate.rearrange("r p t -> p r t")

        nc.sync.dma_start(offs_t[:], offs)

        tables = []
        for g in range(G):
            table = ring.tile([P, 2, 2 * T], BF16, name="table%d" % g, tag="t12", bufs=2, align_bytes=64)
            tables.append(table)

        def raw_tile(name, width):
            return ring.tile([P, 2, width], F32, name=name, tag="raw", bufs=7, align_bytes=64)

        def load_and_cast_x(g, u, t0, width, cut, engine):
            raw = raw_tile("xraw", width)
            for c in range(0, width, cut):
                nc.sync.dma_start(raw[:, :, c : c + cut], x_view[g, :, 2 * u : 2 * u + 2, t0 + c : t0 + c + cut])
                dst = tables[g][:, u, 2 * (t0 + c) : 2 * (t0 + c + cut)].rearrange("p (n e) -> p n e", e=2)
                src = raw[:, :, c : c + cut].rearrange("p e n -> p n e")
                if engine == "V":
                    nc.vector.tensor_copy(dst, src)
                else:
                    nc.scalar.copy(dst, src)

        planes = {}

        def gather(g, u, q):
            if u == 0:
                planes[g, q] = ring.tile([P, 2, 2 * SQ], BF16, name="planes", tag="planes", bufs=4, align_bytes=64)
            nc.vector.tensor_copy(
                planes[g, q][:, u, :].bitcast(U32),
                tables[g][:, u, :].bitcast(U32).indirect(offs_t[:, q * SQ // 16 : (q + 1) * SQ // 16]),
            )

        grouped = {}

        def interleave(g, q):
            t = ring.tile([P, 4 * SQ], BF16, name="grouped", tag="grouped", bufs=3, align_bytes=64)
            dst = t[:].bitcast(F32).rearrange("p (n u) -> p n u", u=2)
            src = planes[g, q][:].rearrange("p u m -> p (u m)").bitcast(F32).rearrange("p (u n) -> p n u", u=2)
            nc.scalar.copy(dst, src)
            grouped[g, q] = t

        def quantise_slots(g, q):
            cols = slice(q * SQ, (q + 1) * SQ)
            nc.vector.quantize_mx(out=sc[:, g, cols].bitcast(FP8X4), scales=ss[:, g, cols], in_=grouped[g, q][:])

        wgrouped = {}

        def load_and_cast_w(e0, n, split):
            raw = raw_tile("wraw", n * 4 * N)
            halves = raw[:].rearrange("p a b -> p (a b)").rearrange("p (e g m) -> p e g m", g=G, m=4 * N)
            nc.sync.dma_start(halves.rearrange("p e g (j n) -> p e g j n", j=4), w_view[:, e0 : e0 + n])
            t = ring.tile([P, n, G * 4 * N], BF16, name="wgrouped", tag="wgrouped", bufs=5, align_bytes=64)
            for k in range(0, n, split):
                dst = t[:, k : k + split, :].rearrange("p e (a c i t) -> p (e a) c t i", c=N // 4, i=4, t=4)
                src = halves[:, k : k + split].rearrange("p e g (t c i) -> p (e g) c t i", t=4, i=4)
                if e0 + k in W_VECTOR:
                    nc.vector.tensor_copy(dst, src)
                else:
                    nc.scalar.copy(dst, src)
            wgrouped[e0] = t

        def quantise_w(e0, n, k=0):
            nc.vector.quantize_mx(
                out=wc[:, e0 + k : e0 + k + n].rearrange("p e g n -> p (e g n)").bitcast(FP8X4),
                scales=ws[:, e0 + k : e0 + k + n].rearrange("p e g n -> p (e g n)"),
                in_=wgrouped[e0][:, k : k + n, :].rearrange("p e m -> p (e m)"),
            )

        def multiply(bank, e, codes, scales, cols):
            for g in range(G):
                nc.tensor.matmul_mx(
                    out=bank,
                    lhsT=wc[:, e, g, :].bitcast(FP8X4),
                    lhsT_scale=ws[:, e, g, :],
                    rhs=codes[:, g, cols].bitcast(FP8X4),
                    rhs_scale=scales[:, g, cols],
                    start=(g == 0),
                    stop=(g == G - 1),
                )

        def group_tokens(g, t0, n, on_vector):
            t = ring.tile([P, 4 * n], BF16, name="xgrouped", tag="grouped", bufs=3, align_bytes=64)
            dst = t[:].bitcast(F32).rearrange("p (n u) -> p n u", u=2)
            words = tables[g][:].rearrange("p u m -> p (u m)").bitcast(F32).rearrange("p (u n) -> p n u", u=2)
            if on_vector:
                nc.vector.tensor_copy(dst, words[:, t0 : t0 + n, :])
            else:
                nc.scalar.copy(dst, words[:, t0 : t0 + n, :])
            return t

        def quantise_tokens(t, g, t0, n):
            cols = slice(t0, t0 + n)
            nc.vector.quantize_mx(out=xc[:, g, cols].bitcast(FP8X4), scales=xs[:, g, cols], in_=t[:])

        def token_steps(g, on_vector):
            a = group_tokens(g, 0, 1024, on_vector)
            c = group_tokens(g, 1024, 512, on_vector)
            quantise_tokens(a, g, 0, 1024)
            quantise_tokens(c, g, 1024, 512)

        def expert_bank(e0, n):
            bank = psum.tile([P, 4 * C], F32, name="bank", tag="bank", bufs=4)
            for k in range(n):
                cols = slice((e0 + k) * C, (e0 + k + 1) * C)
                multiply(bank[:, k * C : (k + 1) * C], e0 + k, sc, ss, cols)
            for k in range(n):
                e = e0 + k
                nc.scalar.activation(
                    y[:, e * C : (e + 1) * C], bank[:, k * C : (k + 1) * C], IDENTITY, bias=b_t[:, e : e + 1]
                )

        load_and_cast_x(0, 0, 0, 1024, 512, "V")
        load_and_cast_x(0, 0, 1024, 512, 256, "V")
        load_and_cast_x(0, 1, 0, 1024, 512, "S")
        load_and_cast_x(0, 1, 1024, 512, 512, "S")
        load_and_cast_x(1, 0, 0, 1024, 1024, "S")
        load_and_cast_x(1, 0, 1024, 512, 512, "S")
        load_and_cast_x(1, 1, 0, 1024, 1024, "S")
        load_and_cast_x(1, 1, 1024, 512, 512, "S")
        nc.sync.dma_start(b_t[:], b)
        nc.sync.dma_start(pos1_t[:], pos1)
        nc.sync.dma_start(pos2_t[:], pos2)

        for u in range(2):
            for q in range(Q):
                gather(0, u, q)
        for q in range(Q):
            interleave(0, q)
        pairs = E // 2
        gates = []
        cuts = ((0, 1024), (1024, 1536))
        for i in range(3):
            load_and_cast_w(2 * i, 2, 2)
        for i in range(2):
            quantise_w(2 * i, 2)
        for q in range(Q):
            gather(1, 0, q)
            gather(1, 1, q)
            interleave(1, q)
            quantise_slots(0, q)
            load_and_cast_w(2 * (3 + q), 2, 2)
            quantise_w(2 * (2 + q), 2)
        for q in range(Q):
            quantise_slots(1, q)
        token_steps(0, True)
        y = ring.tile([P, S], F32, name="y", tag="t12", bufs=2, align_bytes=64)
        for i in range(6, pairs):
            if i == 9:
                load_and_cast_w(E, 1, 1)
                for t0, t1 in cuts:
                    t = raw_tile("gates", t1 - t0)
                    nc.sync.dma_start(t[:], gate_view[:, :, t0:t1])
                    gates.append(t)
            load_and_cast_w(2 * i, 2, 2 if i < pairs - 1 else 1)
            quantise_w(2 * (i - 1), 2)
            if i == 6:
                expert_bank(0, 4)
                expert_bank(4, 4)
            elif i % 2 == 1:
                expert_bank(2 * (i - 3), 4)
        quantise_w(E - 2, 1)
        quantise_w(E - 2, 1, 1)
        expert_bank(20, 2)
        expert_bank(22, 2)
        token_steps(1, True)
        quantise_w(E, 1)
        shared = []
        for c in range(3):
            bank = psum.tile([P, 512], F32, name="shared%d" % c)
            multiply(bank[:], E, xc, xs, slice(c * 512, (c + 1) * 512))
            shared.append(bank)

        first = ring.tile([P, T], F32, name="first", tag="planes", bufs=4, align_bytes=64)
        second = ring.tile([P, T], F32, name="second", tag="planes", bufs=4, align_bytes=64)
        total = ring.tile([P, T], F32, name="total", tag="planes", bufs=4, align_bytes=64)

        def fetch(dst, pos, r, k):
            t0, t1 = cuts[k]
            nc.vector.tensor_tensor(dst[:, t0:t1], y[:].indirect(pos[:, t0 // 16 : t1 // 16]), gates[k][:, r, :], MULT)

        def add_shared(t0, t1):
            c = t0 // 512
            nc.vector.scalar_tensor_tensor(
                out=total[:, t0:t1],
                in0=shared[c][:, t0 - 512 * c : t1 - 512 * c],
                scalar=b_t[:, E : E + 1],
                in1=first[:, t0:t1],
                op0=ADD,
                op1=ADD,
            )

        def add_second(t0, t1):
            nc.vector.tensor_tensor(total[:, t0:t1], total[:, t0:t1], second[:, t0:t1], ADD)
            nc.sync.dma_start(out[:, t0:t1], total[:, t0:t1])

        fetch(first, pos1_t, 0, 0)
        fetch(second, pos2_t, 1, 0)
        add_shared(0, 512)
        add_shared(512, 1024)
        fetch(first, pos1_t, 0, 1)
        add_second(0, 1024)
        fetch(second, pos2_t, 1, 1)
        add_shared(1024, 1280)
        add_shared(1280, 1536)
        add_second(1024, 1280)
        add_second(1280, 1536)
